import numpy as np
import ml_dtypes


def mxq(x, axis, fmt="e4m3"):
    dtype, down = {"e4m3": (ml_dtypes.float8_e4m3fn, 7), "e5m2": (ml_dtypes.float8_e5m2, 14)}[fmt]
    v = np.moveaxis(np.asarray(x, np.float32).astype(ml_dtypes.bfloat16).astype(np.float64), axis, -1)
    blocks = v.reshape(v.shape[:-1] + (-1, 32))
    amax = np.abs(blocks).max(-1, keepdims=True)
    byte = np.maximum(np.where(amax > 0, np.frexp(amax)[1] - 1 + 127, 0) - down, 1)
    scale = np.exp2(byte - 127.0)
    codes = (blocks / scale).astype(np.float32).astype(dtype).astype(np.float64)
    return np.moveaxis((codes * scale).reshape(v.shape), -1, axis)


WIDE = False


def mx_kscale(k):
    if not WIDE:
        return np.ones(k)
    levels = np.array([30, -30])
    if k % 512:
        return np.exp2(np.random.permutation(np.resize(levels, k // 32))).repeat(32)
    a = np.empty((k // 512, 16))
    for p in range(k // 512):
        a[p, :8] = np.random.permutation(np.resize(levels, 8))
        for g in range(8):
            far = levels[np.abs(levels - a[p, g]) >= 10]
            a[p, g + 8] = far[np.random.randint(len(far))]
    return np.exp2(a.ravel()).repeat(32)


def f64(x):
    return np.asarray(x).astype(np.float64)


def striped(idx):
    return np.tile(np.asarray(idx).reshape(-1, 16).T, (8, 1)).astype(np.uint16)


def unstriped(offs):
    return offs[:16].T.reshape(-1).astype(np.int64)


E2M1 = np.array([0.0, 0.5, 1.0, 1.5, 2.0, 3.0, 4.0, 6.0, -0.0, -0.5, -1.0, -1.5, -2.0, -3.0, -4.0, -6.0])


def pack_weight(w, fmt):
    k, n = w.shape
    w = f64(np.asarray(w, np.float32).astype(ml_dtypes.bfloat16)).reshape(k // 32, 32, n)
    amax = np.abs(w).max(1)
    if fmt == "e4m3":
        byte = np.frexp(amax)[1] - 1 + 127 - 7
    else:
        mant, ex = np.frexp(amax / 6.0)
        byte = np.where(mant > 0.5, ex, ex - 1) + 127
    byte = np.clip(np.where(amax > 0, byte, 1), 1, 254)
    scaled = (w * np.exp2(127.0 - byte)[:, None, :]).reshape(k, n).astype(np.float32)
    by_word = np.ascontiguousarray(scaled.reshape(k // 512, 128, 4, n).transpose(0, 1, 3, 2))
    if fmt == "e4m3":
        words = by_word.astype(ml_dtypes.float8_e4m3fn).view(np.uint8)
    else:
        c = by_word.astype(ml_dtypes.float4_e2m1fn).view(np.uint8) & 0xF
        words = (c[..., 0::2] | (c[..., 1::2] << 4)).reshape(k // 512, 128, 2 * n)
    return np.ascontiguousarray(words), np.ascontiguousarray(byte.astype(np.uint8).reshape(k // 512, 16, n))


def unpack_weight(words, scales, fmt):
    g, _, n = scales.shape
    words = np.ascontiguousarray(words).reshape(g, 128, n, -1)
    if fmt == "e4m3":
        vals = words.view(ml_dtypes.float8_e4m3fn).astype(np.float64)
    else:
        nib = np.empty((g, 128, n, 4), np.uint8)
        nib[..., 0::2] = words & 0xF
        nib[..., 1::2] = words >> 4
        vals = E2M1[nib]
    vals = vals * np.repeat(np.exp2(scales.astype(np.float64) - 127.0), 8, axis=1)[..., None]
    return vals.transpose(0, 1, 3, 2).reshape(g * 512, n)


K, R, N, T, J = 512, 512, 512, 1024, 512


def setup_inputs():
    n = np.random.standard_normal
    idx = np.random.permutation(T)[:J]
    fn = mx_kscale(N)
    fr = mx_kscale(R)
    wdp = pack_weight(n((N, R)) * 1 / np.sqrt(N) * fn[:, None], "e2m1")
    wup = pack_weight(n((R, K)) * 1 / np.sqrt(R) / fr[:, None], "e4m3")
    return {
        "g": (n((N, T)) * np.exp(0.5 * n((1, T))) / fn[:, None]).astype(np.float32),
        "wd_words": wdp[0],
        "wd_scales": wdp[1],
        "z": (n((R, T)) * fr[:, None]).astype(np.float32),
        "wu_words": wup[0],
        "wu_scales": wup[1],
        "run": (1.0 * n((K, T))).astype(np.float32),
        "offs": striped(idx),
    }


def reference(g, wd_words, wd_scales, z, wu_words, wu_scales, run, offs):
    idx = unstriped(offs)
    wdu = unpack_weight(wd_words, wd_scales, "e2m1")
    wuu = unpack_weight(wu_words, wu_scales, "e4m3")
    gidxq = mxq(f64(g)[:, idx], 0, "e5m2")
    dh = wdu.T @ gidxq
    dz = 2.0 * dh * np.maximum(f64(z)[:, idx], 0.0)
    dzq = mxq(dz, 0, "e5m2")
    dx = wuu.T @ dzq
    p = np.zeros((K, T))
    p[:, idx] = dx
    y = p + 0.3 * f64(run)
    return y

@@ -1,0 +1,162 @@
+from contextlib import ExitStack
+
+import concourse.mybir as mybir
+
+K, R, N, T, J = 512, 512, 512, 1024, 512
+FLOPS = 2 * N * R * J + 2 * R * K * J
+
+F32 = mybir.dt.float32
+BF16 = mybir.dt.bfloat16
+I32 = mybir.dt.int32
+U32 = mybir.dt.uint32
+U16 = mybir.dt.uint16
+U8 = mybir.dt.uint8
+E2M1 = mybir.dt.float4_e2m1fn_x4
+E4M3 = mybir.dt.float8_e4m3fn_x4
+E5M2 = mybir.dt.float8_e5m2_x4
+ALU = mybir.AluOpType
+COPY = mybir.ActivationFunctionType.Copy
+
+P = 128
+PACK = 4
+RUN_SHARE = 0.3
+SCALAR_COLS = 160
+TAIL_PARTS = 4
+
+
+def load_scale_rows(queue, plane, scales):
+    rows = scales[0].bitcast(I32)
+    for q in range(4):
+        queue.dma_start(out=plane[32 * q : 32 * q + 4, :].bitcast(I32), in_=rows[4 * q : 4 * q + 4, :])
+
+
+def tile_list_squared_relu_back_kernel(tc, g, wd_words, wd_scales, z, wu_words, wu_scales, run, offs, out):
+    nc = tc.nc
+    with ExitStack() as ctx:
+        sb = ctx.enter_context(tc.tile_pool(name="sb", bufs=1))
+        ps = ctx.enter_context(tc.psum_pool(name="ps", bufs=1))
+
+        offsets = sb.tile([P, J // 16], U16, name="offsets")
+        wd_raw = sb.tile([P, R], U16, name="wd_raw", align_bytes=64)
+        wd_raw_scale = sb.tile([P, R], U8, name="wd_raw_scale", align_bytes=64)
+        wd_code = sb.tile([P, R], U16, name="wd_code", align_bytes=64)
+        wd_scale = sb.tile([P, R], U8, name="wd_scale", align_bytes=64)
+        wu_code = sb.tile([P, K], U32, name="wu_code", align_bytes=64)
+        wu_scale = sb.tile([P, K], U8, name="wu_scale", align_bytes=64)
+        g_rows = [sb.tile([P, T], F32, name=f"g_rows{t}") for t in range(PACK)]
+        z_rows = [sb.tile([P, T], F32, name=f"z_rows{t}") for t in range(PACK)]
+        run_rows = [sb.tile([P, T], F32, name=f"run_rows{b}") for b in range(K // P)]
+        page = [sb.tile([P, T], F32, name=f"page{b}") for b in range(K // P)]
+
+        nc.vector.memset(wd_raw_scale[:].bitcast(U32), 0)
+        nc.vector.memset(wu_scale[:].bitcast(U32), 0)
+
+        nc.sync.dma_start(offsets[:], offs)
+        nc.sync.dma_start(out=wd_raw[:].bitcast(I32), in_=wd_words[0].bitcast(I32))
+        load_scale_rows(nc.scalar, wd_raw_scale, wd_scales)
+        g_by_t = g.rearrange("(p t) c -> t p c", t=PACK)
+        z_by_t = z.rearrange("(p t) c -> t p c", t=PACK)
+        for t in range(PACK):
+            nc.sync.dma_start(out=g_rows[t][:], in_=g_by_t[t])
+        for t in range(PACK):
+            nc.sync.dma_start(out=z_rows[t][:], in_=z_by_t[t])
+        nc.sync.dma_start(out=wu_code[:].bitcast(I32), in_=wu_words[0].rearrange("p c t -> p (c t)").bitcast(I32))
+        load_scale_rows(nc.sync, wu_scale, wu_scales)
+        for b in range(K // P):
+            nc.sync.dma_start(out=run_rows[b][:], in_=run[b * P : (b + 1) * P, :])
+
+        for b in range(K // P):
+            nc.vector.memset(page[b][:], 0.0)
+
+        nc.vector.tensor_copy(
+            out=wd_code[:].rearrange("p (t m) -> p t m", t=PACK), in_=wd_raw[:].rearrange("p (m t) -> p t m", t=PACK)
+        )
+        nc.vector.tensor_copy(
+            out=wd_scale[:].rearrange("p (t m) -> p t m", t=PACK),
+            in_=wd_raw_scale[:].rearrange("p (m t) -> p t m", t=PACK),
+        )
+
+        g_picked = sb.tile([P, PACK, J], F32, name="g_picked")
+        for t in range(PACK):
+            nc.vector.tensor_copy(g_picked[:, t, :], g_rows[t][:].indirect(offsets[:]))
+        g_woven = sb.tile([P, J, PACK], BF16, name="g_woven", align_bytes=64)
+        nc.scalar.copy(
+            out=g_woven[:].rearrange("p (c i) t -> p c t i", i=2),
+            in_=g_picked[:].rearrange("p t (c i) -> p c t i", i=2),
+        )
+        z_picked = [sb.tile([P, J], F32, name=f"z_picked{t}") for t in range(PACK)]
+        for t in range(2):
+            nc.vector.tensor_copy(z_picked[t][:], z_rows[t][:].indirect(offsets[:]))
+        g_code = sb.tile([P, J], U32, name="g_code", align_bytes=64)
+        g_scale = sb.tile([P, J], U8, name="g_scale", align_bytes=64)
+        nc.vector.quantize_mx(
+            out=g_code[:].bitcast(E5M2), scales=g_scale[:], in_=g_woven[:].rearrange("p j t -> p (j t)")
+        )
+        for t in range(2, PACK):
+            nc.vector.tensor_copy(z_picked[t][:], z_rows[t][:].indirect(offsets[:]))
+
+        dz_rows = sb.tile([P, PACK, J], BF16, name="dz_rows", align_bytes=64)
+        for t in range(PACK):
+            dh = ps.tile([P, J], F32, name=f"dh{t}")
+            cols = slice(t * P, (t + 1) * P)
+            nc.tensor.matmul_mx(
+                out=dh[:],
+                lhsT=wd_code[:, cols].bitcast(E2M1),
+                lhsT_scale=wd_scale[:, cols],
+                rhs=g_code[:].bitcast(E5M2),
+                rhs_scale=g_scale[:],
+                start=True,
+                stop=True,
+            )
+            nc.vector.scalar_tensor_tensor(dz_rows[:, t, :], z_picked[t][:], 0.0, dh[:], ALU.max, ALU.mult)
+
+        dz_woven = sb.tile([P, J, PACK], BF16, name="dz_woven", align_bytes=64)
+        for engine_copy, cols in (
+            (nc.scalar.copy, slice(0, SCALAR_COLS)),
+            (nc.vector.tensor_copy, slice(SCALAR_COLS, J)),
+        ):
+            engine_copy(
+                out=dz_woven[:, cols, :].rearrange("p (c i) t -> p c t i", i=4),
+                in_=dz_rows[:, :, cols].rearrange("p t (c i) -> p c t i", i=4),
+            )
+        dz_code = sb.tile([P, J], U32, name="dz_code", align_bytes=64)
+        dz_scale = sb.tile([P, J], U8, name="dz_scale", align_bytes=64)
+        nc.vector.quantize_mx(
+            out=dz_code[:].bitcast(E5M2), scales=dz_scale[:], in_=dz_woven[:].rearrange("p j t -> p (j t)")
+        )
+
+        last = K // P - 1
+        dx_rows = []
+        for b in range(K // P):
+            dx = ps.tile([P, J], F32, name=f"dx{b}")
+            cols = slice(b * P, (b + 1) * P)
+            nc.tensor.matmul_mx(
+                out=dx[:],
+                lhsT=wu_code[:, cols].bitcast(E4M3),
+                lhsT_scale=wu_scale[:, cols],
+                rhs=dz_code[:].bitcast(E5M2),
+                rhs_scale=dz_scale[:],
+                start=True,
+                stop=True,
+            )
+            dx_rows.append(sb.tile([P, J], F32, name=f"dx_rows{b}"))
+            nc.scalar.activation(dx_rows[b][:], dx[:], COPY, scale=2.0)
+
+        for b in range(K // P):
+            nc.vector.tensor_copy(page[b][:].indirect(offsets[:]), dx_rows[b][:])
+            result = sb.tile([P, T], F32, name=f"result{b}")
+            rows = slice(b * P, (b + 1) * P)
+            if b < last:
+                run_share = sb.tile([P, T], F32, name=f"run_share{b}")
+                nc.scalar.activation(run_share[:], run_rows[b][:], COPY, scale=RUN_SHARE)
+                nc.gpsimd.tensor_tensor(result[:], page[b][:], run_share[:], ALU.add)
+                nc.sync.dma_start(out=out[rows, :], in_=result[:])
+            else:
+                width = T // TAIL_PARTS
+                for part in range(TAIL_PARTS):
+                    cols = slice(part * width, (part + 1) * width)
+                    nc.vector.scalar_tensor_tensor(
+                        result[:, cols], run_rows[b][:, cols], RUN_SHARE, page[b][:, cols], ALU.mult, ALU.add
+                    )
+                    queue = nc.sync if part % 2 == 0 else nc.scalar
+                    queue.dma_start(out=out[rows, cols], in_=result[:, cols])

@@ -1,6 +1,7 @@
 from contextlib import ExitStack
 
 import concourse.mybir as mybir
+from concourse.masks import make_identity
 
 K, R, N, T, J = 512, 512, 512, 1024, 512
 FLOPS = 2 * N * R * J + 2 * R * K * J
@@ -20,8 +21,10 @@ COPY = mybir.ActivationFunctionType.Copy
 P = 128
 PACK = 4
 RUN_SHARE = 0.3
-SCALAR_COLS = 160
+SCALAR_COLS = 192
 TAIL_PARTS = 4
+BANK = 512
+TURNED_BLOCKS = 2
 
 
 def load_scale_rows(queue, plane, scales):
@@ -46,10 +49,10 @@ def tile_list_squared_relu_back_kernel(tc, g, wd_words, wd_scales, z, wu_words, 
         g_rows = [sb.tile([P, T], F32, name=f"g_rows{t}") for t in range(PACK)]
         z_rows = [sb.tile([P, T], F32, name=f"z_rows{t}") for t in range(PACK)]
         run_rows = [sb.tile([P, T], F32, name=f"run_rows{b}") for b in range(K // P)]
-        page = [sb.tile([P, T], F32, name=f"page{b}") for b in range(K // P)]
+        page = [sb.tile([P, T], F32, name=f"page{b}") for b in range(TURNED_BLOCKS)]
 
-        nc.vector.memset(wd_raw_scale[:].bitcast(U32), 0)
-        nc.vector.memset(wu_scale[:].bitcast(U32), 0)
+        nc.gpsimd.memset(wd_raw_scale[:].bitcast(U32), 0)
+        nc.gpsimd.memset(wu_scale[:].bitcast(U32), 0)
 
         nc.sync.dma_start(offsets[:], offs)
         nc.sync.dma_start(out=wd_raw[:].bitcast(I32), in_=wd_words[0].bitcast(I32))
@@ -65,8 +68,10 @@ def tile_list_squared_relu_back_kernel(tc, g, wd_words, wd_scales, z, wu_words, 
         for b in range(K // P):
             nc.sync.dma_start(out=run_rows[b][:], in_=run[b * P : (b + 1) * P, :])
 
-        for b in range(K // P):
+        for b in range(TURNED_BLOCKS):
             nc.vector.memset(page[b][:], 0.0)
+        identity = sb.tile([P, P], F32, name="identity")
+        make_identity(nc, identity[:])
 
         nc.vector.tensor_copy(
             out=wd_code[:].rearrange("p (t m) -> p t m", t=PACK), in_=wd_raw[:].rearrange("p (m t) -> p t m", t=PACK)
@@ -97,7 +102,7 @@ def tile_list_squared_relu_back_kernel(tc, g, wd_words, wd_scales, z, wu_words, 
 
         dz_rows = sb.tile([P, PACK, J], BF16, name="dz_rows", align_bytes=64)
         for t in range(PACK):
-            dh = ps.tile([P, J], F32, name=f"dh{t}")
+            dh = ps.tile([P, J], F32, name=f"dh{t}", tag=f"bank{t}")
             cols = slice(t * P, (t + 1) * P)
             nc.tensor.matmul_mx(
                 out=dh[:],
@@ -108,27 +113,42 @@ def tile_list_squared_relu_back_kernel(tc, g, wd_words, wd_scales, z, wu_words, 
                 start=True,
                 stop=True,
             )
-            nc.vector.scalar_tensor_tensor(dz_rows[:, t, :], z_picked[t][:], 0.0, dh[:], ALU.max, ALU.mult)
+            for cols in (slice(0, J),) if t < PACK - 1 else (slice(0, J // 2), slice(J // 2, J)):
+                nc.vector.scalar_tensor_tensor(
+                    dz_rows[:, t, cols], z_picked[t][:, cols], 0.0, dh[:, cols], ALU.max, ALU.mult
+                )
 
-        dz_woven = sb.tile([P, J, PACK], BF16, name="dz_woven", align_bytes=64)
-        for engine_copy, cols in (
-            (nc.scalar.copy, slice(0, SCALAR_COLS)),
-            (nc.vector.tensor_copy, slice(SCALAR_COLS, J)),
+        half_j = J // 2
+        dz_woven = [
+            sb.tile([P, half_j, PACK], BF16, name=f"dz_woven{h}", tag=f"woven_then_page{h}", align_bytes=64)
+            for h in range(2)
+        ]
+        for engine_copy, h, start, stop in (
+            (nc.scalar.copy, 0, 0, SCALAR_COLS),
+            (nc.vector.tensor_copy, 0, SCALAR_COLS, half_j),
+            (nc.vector.tensor_copy, 1, 0, half_j),
         ):
             engine_copy(
-                out=dz_woven[:, cols, :].rearrange("p (c i) t -> p c t i", i=4),
-                in_=dz_rows[:, :, cols].rearrange("p t (c i) -> p c t i", i=4),
+                out=dz_woven[h][:, start:stop, :].rearrange("p (c i) t -> p c t i", i=4),
+                in_=dz_rows[:, :, h * half_j + start : h * half_j + stop].rearrange("p t (c i) -> p c t i", i=4),
             )
         dz_code = sb.tile([P, J], U32, name="dz_code", align_bytes=64)
         dz_scale = sb.tile([P, J], U8, name="dz_scale", align_bytes=64)
-        nc.vector.quantize_mx(
-            out=dz_code[:].bitcast(E5M2), scales=dz_scale[:], in_=dz_woven[:].rearrange("p j t -> p (j t)")
-        )
+        for h in range(2):
+            cols = slice(h * half_j, (h + 1) * half_j)
+            nc.vector.quantize_mx(
+                out=dz_code[:, cols].bitcast(E5M2),
+                scales=dz_scale[:, cols],
+                in_=dz_woven[h][:].rearrange("p j t -> p (j t)"),
+            )
+        for h in range(2):
+            page.append(sb.tile([P, T], F32, name=f"late_page{h}", tag=f"woven_then_page{h}", align_bytes=64))
+            nc.vector.memset(page[-1][:], 0.0)
 
         last = K // P - 1
         dx_rows = []
         for b in range(K // P):
-            dx = ps.tile([P, J], F32, name=f"dx{b}")
+            dx = ps.tile([P, J], F32, name=f"dx{b}", tag=f"bank{b}")
             cols = slice(b * P, (b + 1) * P)
             nc.tensor.matmul_mx(
                 out=dx[:],
@@ -140,23 +160,45 @@ def tile_list_squared_relu_back_kernel(tc, g, wd_words, wd_scales, z, wu_words, 
                 stop=True,
             )
             dx_rows.append(sb.tile([P, J], F32, name=f"dx_rows{b}"))
-            nc.scalar.activation(dx_rows[b][:], dx[:], COPY, scale=2.0)
+            nc.scalar.activation(dx_rows[b][:], dx[:], COPY, scale=2.0 / RUN_SHARE if b < TURNED_BLOCKS else 2.0)
+
+        def turn(bank, source, half, start, stop):
+            for i in range(BANK // P):
+                nc.tensor.matmul(
+                    bank[:, i * P : (i + 1) * P],
+                    lhsT=source[:, half * BANK + i * P : half * BANK + (i + 1) * P],
+                    rhs=identity[:],
+                    start=start and i == 0,
+                    stop=stop and i == BANK // P - 1,
+                    is_transpose=True,
+                )
+
+        halves = range(T // BANK)
+        summed = {}
+        for b in range(TURNED_BLOCKS):
+            for h in halves:
+                summed[b, h] = ps.tile([P, BANK], F32, name=f"summed{b}{h}", tag=f"bank{4 + 2 * b + h}")
+                turn(summed[b, h], run_rows[b], h, True, False)
 
         for b in range(K // P):
             nc.vector.tensor_copy(page[b][:].indirect(offsets[:]), dx_rows[b][:])
             result = sb.tile([P, T], F32, name=f"result{b}")
             rows = slice(b * P, (b + 1) * P)
-            if b < last:
-                run_share = sb.tile([P, T], F32, name=f"run_share{b}")
-                nc.scalar.activation(run_share[:], run_rows[b][:], COPY, scale=RUN_SHARE)
-                nc.gpsimd.tensor_tensor(result[:], page[b][:], run_share[:], ALU.add)
-                nc.sync.dma_start(out=out[rows, :], in_=result[:])
+            if b < TURNED_BLOCKS:
+                turned = sb.tile([P, T], F32, name=f"turned{b}")
+                for h in halves:
+                    turn(summed[b, h], page[b], h, False, True)
+                    nc.scalar.activation(turned[:, h * BANK : (h + 1) * BANK], summed[b, h][:], COPY, scale=RUN_SHARE)
+                for h in halves:
+                    back = ps.tile([P, BANK], F32, name=f"back{b}{h}", tag=f"bank{2 * b + h}")
+                    turn(back, turned, h, True, True)
+                    nc.scalar.copy(result[:, h * BANK : (h + 1) * BANK], back[:])
+                nc.scalar.dma_start(out=out[rows, :], in_=result[:])
             else:
-                width = T // TAIL_PARTS
-                for part in range(TAIL_PARTS):
-                    cols = slice(part * width, (part + 1) * width)
+                width = T // TAIL_PARTS if b == last else T
+                for c in range(0, T, width):
+                    cols = slice(c, c + width)
                     nc.vector.scalar_tensor_tensor(
                         result[:, cols], run_rows[b][:, cols], RUN_SHARE, page[b][:, cols], ALU.mult, ALU.add
                     )
-                    queue = nc.sync if part % 2 == 0 else nc.scalar
-                    queue.dma_start(out=out[rows, cols], in_=result[:, cols])
+                    nc.sync.dma_start(out=out[rows, cols], in_=result[:, cols])

@@ -1,7 +1,6 @@
 from contextlib import ExitStack
 
 import concourse.mybir as mybir
-from concourse.masks import make_identity
 
 K, R, N, T, J = 512, 512, 512, 1024, 512
 FLOPS = 2 * N * R * J + 2 * R * K * J
@@ -23,8 +22,7 @@ PACK = 4
 RUN_SHARE = 0.3
 SCALAR_COLS = 192
 TAIL_PARTS = 4
-BANK = 512
-TURNED_BLOCKS = 2
+EARLY_PAGES = 2
 
 
 def load_scale_rows(queue, plane, scales):
@@ -49,7 +47,7 @@ def tile_list_squared_relu_back_kernel(tc, g, wd_words, wd_scales, z, wu_words, 
         g_rows = [sb.tile([P, T], F32, name=f"g_rows{t}") for t in range(PACK)]
         z_rows = [sb.tile([P, T], F32, name=f"z_rows{t}") for t in range(PACK)]
         run_rows = [sb.tile([P, T], F32, name=f"run_rows{b}") for b in range(K // P)]
-        page = [sb.tile([P, T], F32, name=f"page{b}") for b in range(TURNED_BLOCKS)]
+        page = [sb.tile([P, T], F32, name=f"page{b}") for b in range(EARLY_PAGES)]
 
         nc.gpsimd.memset(wd_raw_scale[:].bitcast(U32), 0)
         nc.gpsimd.memset(wu_scale[:].bitcast(U32), 0)
@@ -68,10 +66,8 @@ def tile_list_squared_relu_back_kernel(tc, g, wd_words, wd_scales, z, wu_words, 
         for b in range(K // P):
             nc.sync.dma_start(out=run_rows[b][:], in_=run[b * P : (b + 1) * P, :])
 
-        for b in range(TURNED_BLOCKS):
+        for b in range(EARLY_PAGES):
             nc.vector.memset(page[b][:], 0.0)
-        identity = sb.tile([P, P], F32, name="identity")
-        make_identity(nc, identity[:])
 
         nc.vector.tensor_copy(
             out=wd_code[:].rearrange("p (t m) -> p t m", t=PACK), in_=wd_raw[:].rearrange("p (m t) -> p t m", t=PACK)
@@ -132,7 +128,7 @@ def tile_list_squared_relu_back_kernel(tc, g, wd_words, wd_scales, z, wu_words, 
                 out=dz_woven[h][:, start:stop, :].rearrange("p (c i) t -> p c t i", i=4),
                 in_=dz_rows[:, :, h * half_j + start : h * half_j + stop].rearrange("p t (c i) -> p c t i", i=4),
             )
-        dz_code = sb.tile([P, J], U32, name="dz_code", align_bytes=64)
+        dz_code = sb.tile([P, J], U32, name="dz_code", tag="code_then_share", align_bytes=64)
         dz_scale = sb.tile([P, J], U8, name="dz_scale", align_bytes=64)
         for h in range(2):
             cols = slice(h * half_j, (h + 1) * half_j)
@@ -160,42 +156,19 @@ def tile_list_squared_relu_back_kernel(tc, g, wd_words, wd_scales, z, wu_words, 
                 stop=True,
             )
             dx_rows.append(sb.tile([P, J], F32, name=f"dx_rows{b}"))
-            nc.scalar.activation(dx_rows[b][:], dx[:], COPY, scale=2.0 / RUN_SHARE if b < TURNED_BLOCKS else 2.0)
+            nc.scalar.activation(dx_rows[b][:], dx[:], COPY, scale=2.0)
 
-        def turn(bank, source, half, start, stop):
-            for i in range(BANK // P):
-                nc.tensor.matmul(
-                    bank[:, i * P : (i + 1) * P],
-                    lhsT=source[:, half * BANK + i * P : half * BANK + (i + 1) * P],
-                    rhs=identity[:],
-                    start=start and i == 0,
-                    stop=stop and i == BANK // P - 1,
-                    is_transpose=True,
-                )
-
-        halves = range(T // BANK)
-        summed = {}
-        for b in range(TURNED_BLOCKS):
-            for h in halves:
-                summed[b, h] = ps.tile([P, BANK], F32, name=f"summed{b}{h}", tag=f"bank{4 + 2 * b + h}")
-                turn(summed[b, h], run_rows[b], h, True, False)
-
+        run_share = sb.tile([P, last, T], F32, name="run_share", tag="code_then_share", align_bytes=64)
         for b in range(K // P):
             nc.vector.tensor_copy(page[b][:].indirect(offsets[:]), dx_rows[b][:])
             result = sb.tile([P, T], F32, name=f"result{b}")
             rows = slice(b * P, (b + 1) * P)
-            if b < TURNED_BLOCKS:
-                turned = sb.tile([P, T], F32, name=f"turned{b}")
-                for h in halves:
-                    turn(summed[b, h], page[b], h, False, True)
-                    nc.scalar.activation(turned[:, h * BANK : (h + 1) * BANK], summed[b, h][:], COPY, scale=RUN_SHARE)
-                for h in halves:
-                    back = ps.tile([P, BANK], F32, name=f"back{b}{h}", tag=f"bank{2 * b + h}")
-                    turn(back, turned, h, True, True)
-                    nc.scalar.copy(result[:, h * BANK : (h + 1) * BANK], back[:])
+            if b < last:
+                nc.scalar.activation(run_share[:, b, :], run_rows[b][:], COPY, scale=RUN_SHARE)
+                nc.gpsimd.tensor_tensor(result[:], page[b][:], run_share[:, b, :], ALU.add)
                 nc.scalar.dma_start(out=out[rows, :], in_=result[:])
             else:
-                width = T // TAIL_PARTS if b == last else T
+                width = T // TAIL_PARTS
                 for c in range(0, T, width):
                     cols = slice(c, c + width)
                     nc.vector.scalar_tensor_tensor(

from contextlib import ExitStack

import concourse.mybir as mybir

K, R, N, T, J = 512, 512, 512, 1024, 512
FLOPS = 2 * N * R * J + 2 * R * K * J

F32 = mybir.dt.float32
BF16 = mybir.dt.bfloat16
I32 = mybir.dt.int32
U32 = mybir.dt.uint32
U16 = mybir.dt.uint16
U8 = mybir.dt.uint8
E2M1 = mybir.dt.float4_e2m1fn_x4
E4M3 = mybir.dt.float8_e4m3fn_x4
E5M2 = mybir.dt.float8_e5m2_x4
ALU = mybir.AluOpType
COPY = mybir.ActivationFunctionType.Copy

P = 128
PACK = 4
RUN_SHARE = 0.3
SCALAR_COLS = 192
TAIL_PARTS = 4
EARLY_PAGES = 2


def load_scale_rows(queue, plane, scales):
    rows = scales[0].bitcast(I32)
    for q in range(4):
        queue.dma_start(out=plane[32 * q : 32 * q + 4, :].bitcast(I32), in_=rows[4 * q : 4 * q + 4, :])


def tile_list_squared_relu_back_kernel(tc, g, wd_words, wd_scales, z, wu_words, wu_scales, run, offs, out):
    nc = tc.nc
    with ExitStack() as ctx:
        sb = ctx.enter_context(tc.tile_pool(name="sb", bufs=1))
        ps = ctx.enter_context(tc.psum_pool(name="ps", bufs=1))

        offsets = sb.tile([P, J // 16], U16, name="offsets")
        wd_raw = sb.tile([P, R], U16, name="wd_raw", align_bytes=64)
        wd_raw_scale = sb.tile([P, R], U8, name="wd_raw_scale", align_bytes=64)
        wd_code = sb.tile([P, R], U16, name="wd_code", align_bytes=64)
        wd_scale = sb.tile([P, R], U8, name="wd_scale", align_bytes=64)
        wu_code = sb.tile([P, K], U32, name="wu_code", align_bytes=64)
        wu_scale = sb.tile([P, K], U8, name="wu_scale", align_bytes=64)
        g_rows = [sb.tile([P, T], F32, name=f"g_rows{t}") for t in range(PACK)]
        z_rows = [sb.tile([P, T], F32, name=f"z_rows{t}") for t in range(PACK)]
        run_rows = [sb.tile([P, T], F32, name=f"run_rows{b}") for b in range(K // P)]
        page = [sb.tile([P, T], F32, name=f"page{b}") for b in range(EARLY_PAGES)]

        nc.gpsimd.memset(wd_raw_scale[:].bitcast(U32), 0)
        nc.gpsimd.memset(wu_scale[:].bitcast(U32), 0)

        nc.sync.dma_start(offsets[:], offs)
        nc.sync.dma_start(out=wd_raw[:].bitcast(I32), in_=wd_words[0].bitcast(I32))
        load_scale_rows(nc.scalar, wd_raw_scale, wd_scales)
        g_by_t = g.rearrange("(p t) c -> t p c", t=PACK)
        z_by_t = z.rearrange("(p t) c -> t p c", t=PACK)
        for t in range(PACK):
            nc.sync.dma_start(out=g_rows[t][:], in_=g_by_t[t])
        for t in range(PACK):
            nc.sync.dma_start(out=z_rows[t][:], in_=z_by_t[t])
        nc.sync.dma_start(out=wu_code[:].bitcast(I32), in_=wu_words[0].rearrange("p c t -> p (c t)").bitcast(I32))
        load_scale_rows(nc.sync, wu_scale, wu_scales)
        for b in range(K // P):
            nc.sync.dma_start(out=run_rows[b][:], in_=run[b * P : (b + 1) * P, :])

        for b in range(EARLY_PAGES):
            nc.vector.memset(page[b][:], 0.0)

        nc.vector.tensor_copy(
            out=wd_code[:].rearrange("p (t m) -> p t m", t=PACK), in_=wd_raw[:].rearrange("p (m t) -> p t m", t=PACK)
        )
        nc.vector.tensor_copy(
            out=wd_scale[:].rearrange("p (t m) -> p t m", t=PACK),
            in_=wd_raw_scale[:].rearrange("p (m t) -> p t m", t=PACK),
        )

        g_picked = sb.tile([P, PACK, J], F32, name="g_picked")
        for t in range(PACK):
            nc.vector.tensor_copy(g_picked[:, t, :], g_rows[t][:].indirect(offsets[:]))
        g_woven = sb.tile([P, J, PACK], BF16, name="g_woven", align_bytes=64)
        nc.scalar.copy(
            out=g_woven[:].rearrange("p (c i) t -> p c t i", i=2),
            in_=g_picked[:].rearrange("p t (c i) -> p c t i", i=2),
        )
        z_picked = [sb.tile([P, J], F32, name=f"z_picked{t}") for t in range(PACK)]
        for t in range(2):
            nc.vector.tensor_copy(z_picked[t][:], z_rows[t][:].indirect(offsets[:]))
        g_code = sb.tile([P, J], U32, name="g_code", align_bytes=64)
        g_scale = sb.tile([P, J], U8, name="g_scale", align_bytes=64)
        nc.vector.quantize_mx(
            out=g_code[:].bitcast(E5M2), scales=g_scale[:], in_=g_woven[:].rearrange("p j t -> p (j t)")
        )
        for t in range(2, PACK):
            nc.vector.tensor_copy(z_picked[t][:], z_rows[t][:].indirect(offsets[:]))

        dz_rows = sb.tile([P, PACK, J], BF16, name="dz_rows", align_bytes=64)
        for t in range(PACK):
            dh = ps.tile([P, J], F32, name=f"dh{t}", tag=f"bank{t}")
            cols = slice(t * P, (t + 1) * P)
            nc.tensor.matmul_mx(
                out=dh[:],
                lhsT=wd_code[:, cols].bitcast(E2M1),
                lhsT_scale=wd_scale[:, cols],
                rhs=g_code[:].bitcast(E5M2),
                rhs_scale=g_scale[:],
                start=True,
                stop=True,
            )
            for cols in (slice(0, J),) if t < PACK - 1 else (slice(0, J // 2), slice(J // 2, J)):
                nc.vector.scalar_tensor_tensor(
                    dz_rows[:, t, cols], z_picked[t][:, cols], 0.0, dh[:, cols], ALU.max, ALU.mult
                )

        half_j = J // 2
        dz_woven = [
            sb.tile([P, half_j, PACK], BF16, name=f"dz_woven{h}", tag=f"woven_then_page{h}", align_bytes=64)
            for h in range(2)
        ]
        for engine_copy, h, start, stop in (
            (nc.scalar.copy, 0, 0, SCALAR_COLS),
            (nc.vector.tensor_copy, 0, SCALAR_COLS, half_j),
            (nc.vector.tensor_copy, 1, 0, half_j),
        ):
            engine_copy(
                out=dz_woven[h][:, start:stop, :].rearrange("p (c i) t -> p c t i", i=4),
                in_=dz_rows[:, :, h * half_j + start : h * half_j + stop].rearrange("p t (c i) -> p c t i", i=4),
            )
        dz_code = sb.tile([P, J], U32, name="dz_code", tag="code_then_share", align_bytes=64)
        dz_scale = sb.tile([P, J], U8, name="dz_scale", align_bytes=64)
        for h in range(2):
            cols = slice(h * half_j, (h + 1) * half_j)
            nc.vector.quantize_mx(
                out=dz_code[:, cols].bitcast(E5M2),
                scales=dz_scale[:, cols],
                in_=dz_woven[h][:].rearrange("p j t -> p (j t)"),
            )
        for h in range(2):
            page.append(sb.tile([P, T], F32, name=f"late_page{h}", tag=f"woven_then_page{h}", align_bytes=64))
            nc.vector.memset(page[-1][:], 0.0)

        last = K // P - 1
        dx_rows = []
        for b in range(K // P):
            dx = ps.tile([P, J], F32, name=f"dx{b}", tag=f"bank{b}")
            cols = slice(b * P, (b + 1) * P)
            nc.tensor.matmul_mx(
                out=dx[:],
                lhsT=wu_code[:, cols].bitcast(E4M3),
                lhsT_scale=wu_scale[:, cols],
                rhs=dz_code[:].bitcast(E5M2),
                rhs_scale=dz_scale[:],
                start=True,
                stop=True,
            )
            dx_rows.append(sb.tile([P, J], F32, name=f"dx_rows{b}"))
            nc.scalar.activation(dx_rows[b][:], dx[:], COPY, scale=2.0)

        run_share = sb.tile([P, last, T], F32, name="run_share", tag="code_then_share", align_bytes=64)
        for b in range(K // P):
            nc.vector.tensor_copy(page[b][:].indirect(offsets[:]), dx_rows[b][:])
            result = sb.tile([P, T], F32, name=f"result{b}")
            rows = slice(b * P, (b + 1) * P)
            if b < last:
                nc.scalar.activation(run_share[:, b, :], run_rows[b][:], COPY, scale=RUN_SHARE)
                nc.gpsimd.tensor_tensor(result[:], page[b][:], run_share[:, b, :], ALU.add)
                nc.scalar.dma_start(out=out[rows, :], in_=result[:])
            else:
                width = T // TAIL_PARTS
                for c in range(0, T, width):
                    cols = slice(c, c + width)
                    nc.vector.scalar_tensor_tensor(
                        result[:, cols], run_rows[b][:, cols], RUN_SHARE, page[b][:, cols], ALU.mult, ALU.add
                    )
                    nc.sync.dma_start(out=out[rows, cols], in_=result[:, cols])
